import numpy as np
import ml_dtypes


def mxq(x, axis, fmt="e4m3"):
    dtype, down = {"e4m3": (ml_dtypes.float8_e4m3fn, 7), "e5m2": (ml_dtypes.float8_e5m2, 14)}[fmt]
    v = np.moveaxis(np.asarray(x, np.float32).astype(ml_dtypes.bfloat16).astype(np.float64), axis, -1)
    blocks = v.reshape(v.shape[:-1] + (-1, 32))
    amax = np.abs(blocks).max(-1, keepdims=True)
    byte = np.maximum(np.where(amax > 0, np.frexp(amax)[1] - 1 + 127, 0) - down, 1)
    scale = np.exp2(byte - 127.0)
    codes = (blocks / scale).astype(np.float32).astype(dtype).astype(np.float64)
    return np.moveaxis((codes * scale).reshape(v.shape), -1, axis)


WIDE = False


def mx_kscale(k):
    if not WIDE:
        return np.ones(k)
    levels = np.array([10, -10, 5, -5, 0])
    if k % 512:
        return np.exp2(np.random.permutation(np.resize(levels, k // 32))).repeat(32)
    a = np.empty((k // 512, 16))
    for p in range(k // 512):
        a[p, :8] = np.random.permutation(np.resize(levels, 8))
        for g in range(8):
            far = levels[np.abs(levels - a[p, g]) >= 10]
            a[p, g + 8] = far[np.random.randint(len(far))]
    return np.exp2(a.ravel()).repeat(32)


def f64(x):
    return np.asarray(x).astype(np.float64)


def striped(idx):
    return np.tile(idx.reshape(-1, 16).T, (8, 1)).astype(np.uint16)


def unstriped(offs):
    return offs[:16].T.reshape(-1).astype(np.int64)


def pack_weight(w):
    k, n = w.shape
    w = f64(np.asarray(w, np.float32).astype(ml_dtypes.bfloat16)).reshape(k // 32, 32, n)
    amax = np.abs(w).max(1)
    byte = np.clip(np.where(amax > 0, np.frexp(amax)[1] - 1 + 127 - 7, 1), 1, 254)
    scaled = (w * np.exp2(127.0 - byte)[:, None, :]).reshape(k, n).astype(np.float32)
    words = np.ascontiguousarray(scaled.reshape(k // 512, 128, 4, n).transpose(0, 1, 3, 2)).astype(ml_dtypes.float8_e4m3fn).view(np.uint8)
    return words, np.ascontiguousarray(byte.astype(np.uint8).reshape(k // 512, 16, n))


def unpack_weight(words, scales):
    g, p, n, _ = words.shape
    vals = np.ascontiguousarray(words).view(ml_dtypes.float8_e4m3fn).astype(np.float64) * np.repeat(np.exp2(scales.astype(np.float64) - 127.0), 8, axis=1)[..., None]
    return vals.transpose(0, 1, 3, 2).reshape(g * 512, n)


K, T, E, C, N = 512, 2048, 8, 256, 128


def by_expert(wq, xq):
    return np.concatenate([wq[e].T @ xq[:, e * C:(e + 1) * C] for e in range(E)], axis=1)


def setup_inputs():
    n = np.random.standard_normal
    s = mx_kscale(K)[:, None]
    packed = [pack_weight(m) for m in n((E, K, N)) / np.sqrt(K) / s[None]]
    return {
        "xT": (n((K, T)) * s).astype(np.float32),
        "w_words": np.stack([m[0] for m in packed]),
        "w_scales": np.stack([m[1] for m in packed]),
        "gate": np.tile(np.random.uniform(0.2, 1.0, E * C), (N, 1)).astype(np.float32),
        "offs": striped(np.random.permutation(T)[:E * C]),
    }


def reference(xT, w_words, w_scales, gate, offs):
    idx = unstriped(offs)
    xq = mxq(f64(xT)[:, idx], 0, "e4m3")
    w = np.stack([unpack_weight(w_words[e], w_scales[e]) for e in range(E)])
    y = by_expert(w, xq)
    out = np.zeros((N, T))
    out[:, idx] = f64(gate) * y
    return out

@@ -1,0 +1,114 @@
+from contextlib import ExitStack
+
+import concourse.mybir as mybir
+
+K, T, E, C, N = 512, 2048, 8, 256, 128
+FLOPS = 2 * K * N * E * C
+
+F32 = mybir.dt.float32
+BF16 = mybir.dt.bfloat16
+U32 = mybir.dt.uint32
+I32 = mybir.dt.int32
+U16 = mybir.dt.uint16
+U8 = mybir.dt.uint8
+FP8X4 = mybir.dt.float8_e4m3fn_x4
+MULT = mybir.AluOpType.mult
+
+P = 128
+PACK = 4
+CHUNK = 512
+CHUNKS = E * C // CHUNK
+OFF_COLS = CHUNK // 16
+
+
+def tile_routed_moe_kernel(tc, xT, w_words, w_scales, gate, offs, out):
+    nc = tc.nc
+    with ExitStack() as ctx:
+        held = ctx.enter_context(tc.tile_pool(name="held", bufs=1))
+        psum = ctx.enter_context(tc.psum_pool(name="psum", bufs=1))
+
+        offsets = held.tile([P, E * C // 16], U16, name="offsets")
+        nc.sync.dma_start(offsets[:], offs)
+
+        x_view = xT.rearrange("(p t) n -> p t n", t=PACK)
+        planes = []
+        for t in range(PACK):
+            plane = held.tile([P, T], F32, name="plane%d" % t)
+            nc.sync.dma_start(plane[:], x_view[:, t, :])
+            planes.append(plane)
+
+        w_codes = held.tile([P, E, N], U32, name="w_codes", align_bytes=64)
+        nc.sync.dma_start(
+            w_codes[:].bitcast(I32),
+            w_words.rearrange("e a p n r -> p (e a) (n r)").bitcast(I32),
+        )
+        w_planes = held.tile([P, E, N], U8, name="w_planes", align_bytes=64)
+        nc.vector.memset(w_planes[:].rearrange("p e n -> p (e n)").bitcast(I32), 0)
+        for q in range(4):
+            nc.sync.dma_start(
+                w_planes[32 * q : 32 * q + 4, :, :].bitcast(I32),
+                w_scales[:, 0, 4 * q : 4 * q + 4, :].rearrange("e r n -> r e n").bitcast(I32),
+            )
+        gate_sb = held.tile([P, E * C], F32, name="gate_sb")
+        nc.sync.dma_start(gate_sb[:], gate)
+
+        window = held.tile([P, T], F32, name="window")
+
+        gathered = [held.tile([P, PACK, CHUNK], F32, name="gathered%d" % c) for c in range(CHUNKS)]
+        grouped = [held.tile([P, CHUNK, PACK], BF16, name="grouped%d" % c, align_bytes=64) for c in range(CHUNKS)]
+        codes = [held.tile([P, CHUNK], U32, name="codes%d" % c, align_bytes=64) for c in range(CHUNKS)]
+        scales = [held.tile([P, CHUNK], U8, name="scales%d" % c, align_bytes=64) for c in range(CHUNKS)]
+        sums = [held.tile([P, CHUNK], F32, name="sums%d" % c) for c in range(CHUNKS)]
+        banks = [psum.tile([P, CHUNK], F32, name="bank%d" % c) for c in range(CHUNKS)]
+
+        def chunk_offsets(c):
+            return offsets[:, c * OFF_COLS : (c + 1) * OFF_COLS]
+
+        def gather(t, c):
+            nc.vector.tensor_copy(gathered[c][:, t, :], planes[t][:].indirect(chunk_offsets(c)))
+
+        def interleave(c):
+            nc.scalar.copy(grouped[c][:], gathered[c][:].rearrange("p t n -> p n t"))
+
+        def quantize_and_multiply(c):
+            nc.vector.quantize_mx(
+                out=codes[c][:].bitcast(FP8X4),
+                scales=scales[c][:],
+                in_=grouped[c][:].rearrange("p n t -> p (n t)"),
+            )
+            for h in range(CHUNK // C):
+                e = c * (CHUNK // C) + h
+                cols = slice(h * C, (h + 1) * C)
+                nc.tensor.matmul_mx(
+                    out=banks[c][:, cols],
+                    lhsT=w_codes[:, e, :].bitcast(FP8X4),
+                    lhsT_scale=w_planes[:, e, :],
+                    rhs=codes[c][:, cols].bitcast(FP8X4),
+                    rhs_scale=scales[c][:, cols],
+                    start=True,
+                    stop=True,
+                )
+            nc.scalar.copy(sums[c][:], banks[c][:])
+
+        def scatter(c):
+            nc.vector.tensor_tensor(
+                window[:].indirect(chunk_offsets(c)),
+                sums[c][:],
+                gate_sb[:, c * CHUNK : (c + 1) * CHUNK],
+                MULT,
+            )
+
+        for c in range(CHUNKS):
+            gather(0, c)
+        for c in range(CHUNKS):
+            for t in range(1, PACK):
+                gather(t, c)
+            interleave(c)
+            if c >= 1:
+                quantize_and_multiply(c - 1)
+        scatter(0)
+        quantize_and_multiply(CHUNKS - 1)
+        for c in range(1, CHUNKS):
+            scatter(c)
+
+        nc.sync.dma_start(out, window[:])

@@ -13,12 +13,14 @@ U16 = mybir.dt.uint16
 U8 = mybir.dt.uint8
 FP8X4 = mybir.dt.float8_e4m3fn_x4
 MULT = mybir.AluOpType.mult
+COPY = mybir.ActivationFunctionType.Copy
 
 P = 128
 PACK = 4
 CHUNK = 512
 CHUNKS = E * C // CHUNK
 OFF_COLS = CHUNK // 16
+HALF = T // 2
 
 
 def tile_routed_moe_kernel(tc, xT, w_words, w_scales, gate, offs, out):
@@ -31,11 +33,14 @@ def tile_routed_moe_kernel(tc, xT, w_words, w_scales, gate, offs, out):
         nc.sync.dma_start(offsets[:], offs)
 
         x_view = xT.rearrange("(p t) n -> p t n", t=PACK)
-        planes = []
-        for t in range(PACK):
-            plane = held.tile([P, T], F32, name="plane%d" % t)
-            nc.sync.dma_start(plane[:], x_view[:, t, :])
-            planes.append(plane)
+        low = held.tile([P, 2, T], F32, name="low")
+        staged = {}
+        nc.sync.dma_start(low[:, 0, :], x_view[:, 0, :])
+        for t in (2, 3):
+            for h in range(2):
+                staged[t, h] = held.tile([P, HALF], F32, name="staged%d_%d" % (t, h))
+                nc.sync.dma_start(staged[t, h][:], x_view[:, t, h * HALF : (h + 1) * HALF])
+        nc.sync.dma_start(low[:, 1, :], x_view[:, 1, :])
 
         w_codes = held.tile([P, E, N], U32, name="w_codes", align_bytes=64)
         nc.sync.dma_start(
@@ -53,8 +58,8 @@ def tile_routed_moe_kernel(tc, xT, w_words, w_scales, gate, offs, out):
         nc.sync.dma_start(gate_sb[:], gate)
 
         window = held.tile([P, T], F32, name="window")
+        high = held.tile([P, 2, T], BF16, name="high")
 
-        gathered = [held.tile([P, PACK, CHUNK], F32, name="gathered%d" % c) for c in range(CHUNKS)]
         grouped = [held.tile([P, CHUNK, PACK], BF16, name="grouped%d" % c, align_bytes=64) for c in range(CHUNKS)]
         codes = [held.tile([P, CHUNK], U32, name="codes%d" % c, align_bytes=64) for c in range(CHUNKS)]
         scales = [held.tile([P, CHUNK], U8, name="scales%d" % c, align_bytes=64) for c in range(CHUNKS)]
@@ -64,11 +69,11 @@ def tile_routed_moe_kernel(tc, xT, w_words, w_scales, gate, offs, out):
         def chunk_offsets(c):
             return offsets[:, c * OFF_COLS : (c + 1) * OFF_COLS]
 
-        def gather(t, c):
-            nc.vector.tensor_copy(gathered[c][:, t, :], planes[t][:].indirect(chunk_offsets(c)))
+        def gather_low(t, c):
+            nc.vector.tensor_copy(grouped[c][:, :, t], low[:, t, :].indirect(chunk_offsets(c)))
 
-        def interleave(c):
-            nc.scalar.copy(grouped[c][:], gathered[c][:].rearrange("p t n -> p n t"))
+        def gather_high(t, c):
+            nc.scalar.activation(grouped[c][:, :, t], high[:, t - 2, :].indirect(chunk_offsets(c)), COPY)
 
         def quantize_and_multiply(c):
             nc.vector.quantize_mx(
@@ -88,7 +93,6 @@ def tile_routed_moe_kernel(tc, xT, w_words, w_scales, gate, offs, out):
                     start=True,
                     stop=True,
                 )
-            nc.scalar.copy(sums[c][:], banks[c][:])
 
         def scatter(c):
             nc.vector.tensor_tensor(
@@ -98,17 +102,33 @@ def tile_routed_moe_kernel(tc, xT, w_words, w_scales, gate, offs, out):
                 MULT,
             )
 
+        for h in range(2):
+            nc.scalar.copy(high[:, 0, h * HALF : (h + 1) * HALF], staged[2, h][:])
         for c in range(CHUNKS):
-            gather(0, c)
+            gather_low(0, c)
+        for h in range(2):
+            nc.vector.tensor_copy(high[:, 1, h * HALF : (h + 1) * HALF], staged[3, h][:])
         for c in range(CHUNKS):
-            for t in range(1, PACK):
-                gather(t, c)
-            interleave(c)
-            if c >= 1:
-                quantize_and_multiply(c - 1)
+            gather_low(1, c)
+        gather_high(2, 0)
+        gather_high(2, 1)
+        gather_high(3, 0)
+        gather_high(3, 1)
+        for c in (2, 3):
+            gather_high(2, c)
+            gather_high(3, c)
+
+        quantize_and_multiply(0)
+        quantize_and_multiply(1)
+        nc.vector.tensor_copy(sums[0][:], banks[0][:])
         scatter(0)
-        quantize_and_multiply(CHUNKS - 1)
-        for c in range(1, CHUNKS):
-            scatter(c)
+        quantize_and_multiply(2)
+        nc.vector.tensor_copy(sums[1][:], banks[1][:])
+        scatter(1)
+        quantize_and_multiply(3)
+        nc.scalar.copy(sums[2][:], banks[2][:])
+        scatter(2)
+        nc.scalar.copy(sums[3][:], banks[3][:])
+        scatter(3)
 
         nc.sync.dma_start(out, window[:])

@@ -19,7 +19,6 @@ P = 128
 PACK = 4
 CHUNK = 512
 CHUNKS = E * C // CHUNK
-OFF_COLS = CHUNK // 16
 HALF = T // 2
 
 
@@ -60,26 +59,30 @@ def tile_routed_moe_kernel(tc, xT, w_words, w_scales, gate, offs, out):
         window = held.tile([P, T], F32, name="window")
         high = held.tile([P, 2, T], BF16, name="high")
 
-        grouped = [held.tile([P, CHUNK, PACK], BF16, name="grouped%d" % c, align_bytes=64) for c in range(CHUNKS)]
-        codes = [held.tile([P, CHUNK], U32, name="codes%d" % c, align_bytes=64) for c in range(CHUNKS)]
+        grouped = [held.tile([P, HALF, PACK], BF16, name="grouped%d" % h, align_bytes=64) for h in range(2)]
         scales = [held.tile([P, CHUNK], U8, name="scales%d" % c, align_bytes=64) for c in range(CHUNKS)]
-        sums = [held.tile([P, CHUNK], F32, name="sums%d" % c) for c in range(CHUNKS)]
         banks = [psum.tile([P, CHUNK], F32, name="bank%d" % c) for c in range(CHUNKS)]
 
-        def chunk_offsets(c):
-            return offsets[:, c * OFF_COLS : (c + 1) * OFF_COLS]
+        def slot_offsets(first, count):
+            return offsets[:, first // 16 : (first + count) // 16]
 
-        def gather_low(t, c):
-            nc.vector.tensor_copy(grouped[c][:, :, t], low[:, t, :].indirect(chunk_offsets(c)))
+        def gather_low(t, h):
+            nc.vector.tensor_copy(grouped[h][:, :, t], low[:, t, :].indirect(slot_offsets(h * HALF, HALF)))
+
+        def chunk_of_grouped(c):
+            first = (c % 2) * CHUNK
+            return grouped[c // 2][:, first : first + CHUNK, :]
 
         def gather_high(t, c):
-            nc.scalar.activation(grouped[c][:, :, t], high[:, t - 2, :].indirect(chunk_offsets(c)), COPY)
+            nc.scalar.activation(
+                chunk_of_grouped(c)[:, :, t], high[:, t - 2, :].indirect(slot_offsets(c * CHUNK, CHUNK)), COPY
+            )
 
-        def quantize_and_multiply(c):
+        def quantize_and_multiply(c, codes):
             nc.vector.quantize_mx(
-                out=codes[c][:].bitcast(FP8X4),
+                out=codes[:].bitcast(FP8X4),
                 scales=scales[c][:],
-                in_=grouped[c][:].rearrange("p n t -> p (n t)"),
+                in_=chunk_of_grouped(c).rearrange("p n t -> p (n t)"),
             )
             for h in range(CHUNK // C):
                 e = c * (CHUNK // C) + h
@@ -88,47 +91,55 @@ def tile_routed_moe_kernel(tc, xT, w_words, w_scales, gate, offs, out):
                     out=banks[c][:, cols],
                     lhsT=w_codes[:, e, :].bitcast(FP8X4),
                     lhsT_scale=w_planes[:, e, :],
-                    rhs=codes[c][:, cols].bitcast(FP8X4),
+                    rhs=codes[:, cols].bitcast(FP8X4),
                     rhs_scale=scales[c][:, cols],
                     start=True,
                     stop=True,
                 )
 
-        def scatter(c):
+        def scatter(c, sums):
             nc.vector.tensor_tensor(
-                window[:].indirect(chunk_offsets(c)),
-                sums[c][:],
+                window[:].indirect(slot_offsets(c * CHUNK, CHUNK)),
+                sums[:],
                 gate_sb[:, c * CHUNK : (c + 1) * CHUNK],
                 MULT,
             )
 
         for h in range(2):
             nc.scalar.copy(high[:, 0, h * HALF : (h + 1) * HALF], staged[2, h][:])
-        for c in range(CHUNKS):
-            gather_low(0, c)
-        for h in range(2):
-            nc.vector.tensor_copy(high[:, 1, h * HALF : (h + 1) * HALF], staged[3, h][:])
-        for c in range(CHUNKS):
-            gather_low(1, c)
+        gather_low(0, 0)
+        gather_low(0, 1)
+        nc.vector.tensor_copy(high[:, 1, 0:HALF], staged[3, 0][:])
         gather_high(2, 0)
-        gather_high(2, 1)
+        nc.scalar.copy(high[:, 1, HALF:T], staged[3, 1][:])
         gather_high(3, 0)
+        gather_high(2, 1)
         gather_high(3, 1)
+        gather_low(1, 0)
+        gather_low(1, 1)
         for c in (2, 3):
             gather_high(2, c)
             gather_high(3, c)
 
-        quantize_and_multiply(0)
-        quantize_and_multiply(1)
-        nc.vector.tensor_copy(sums[0][:], banks[0][:])
-        scatter(0)
-        quantize_and_multiply(2)
-        nc.vector.tensor_copy(sums[1][:], banks[1][:])
-        scatter(1)
-        quantize_and_multiply(3)
-        nc.scalar.copy(sums[2][:], banks[2][:])
-        scatter(2)
-        nc.scalar.copy(sums[3][:], banks[3][:])
-        scatter(3)
+        codes0 = held.tile([P, CHUNK], U32, name="codes0", align_bytes=64)
+        quantize_and_multiply(0, codes0)
+        codes1 = held.tile([P, CHUNK], U32, name="codes1", align_bytes=64)
+        quantize_and_multiply(1, codes1)
+        sums0 = held.tile([P, CHUNK], F32, name="sums0", tag="swap0", align_bytes=64)
+        nc.vector.tensor_copy(sums0[:], banks[0][:])
+        sums1 = held.tile([P, CHUNK], F32, name="sums1", tag="swap1", align_bytes=64)
+        nc.vector.tensor_copy(sums1[:], banks[1][:])
+        scatter(0, sums0)
+        codes2 = held.tile([P, CHUNK], U32, name="codes2", tag="swap0", align_bytes=64)
+        quantize_and_multiply(2, codes2)
+        scatter(1, sums1)
+        codes3 = held.tile([P, CHUNK], U32, name="codes3", tag="swap1", align_bytes=64)
+        quantize_and_multiply(3, codes3)
+        sums2 = held.tile([P, CHUNK], F32, name="sums2")
+        nc.scalar.copy(sums2[:], banks[2][:])
+        scatter(2, sums2)
+        sums3 = held.tile([P, CHUNK], F32, name="sums3")
+        nc.scalar.copy(sums3[:], banks[3][:])
+        scatter(3, sums3)
 
         nc.sync.dma_start(out, window[:])

@@ -41,11 +41,6 @@ def tile_routed_moe_kernel(tc, xT, w_words, w_scales, gate, offs, out):
                 nc.sync.dma_start(staged[t, h][:], x_view[:, t, h * HALF : (h + 1) * HALF])
         nc.sync.dma_start(low[:, 1, :], x_view[:, 1, :])
 
-        w_codes = held.tile([P, E, N], U32, name="w_codes", align_bytes=64)
-        nc.sync.dma_start(
-            w_codes[:].bitcast(I32),
-            w_words.rearrange("e a p n r -> p (e a) (n r)").bitcast(I32),
-        )
         w_planes = held.tile([P, E, N], U8, name="w_planes", align_bytes=64)
         nc.vector.memset(w_planes[:].rearrange("p e n -> p (e n)").bitcast(I32), 0)
         for q in range(4):
@@ -54,7 +49,13 @@ def tile_routed_moe_kernel(tc, xT, w_words, w_scales, gate, offs, out):
                 w_scales[:, 0, 4 * q : 4 * q + 4, :].rearrange("e r n -> r e n").bitcast(I32),
             )
         gate_sb = held.tile([P, E * C], F32, name="gate_sb")
-        nc.sync.dma_start(gate_sb[:], gate)
+        nc.sync.dma_start(gate_sb[:, 0:CHUNK], gate[:, 0:CHUNK])
+        w_codes = held.tile([P, E, N], U32, name="w_codes", align_bytes=64)
+        nc.sync.dma_start(
+            w_codes[:].bitcast(I32),
+            w_words.rearrange("e a p n r -> p (e a) (n r)").bitcast(I32),
+        )
+        nc.sync.dma_start(gate_sb[:, CHUNK : E * C], gate[:, CHUNK : E * C])
 
         window = held.tile([P, T], F32, name="window")
         high = held.tile([P, 2, T], BF16, name="high")
@@ -66,8 +67,11 @@ def tile_routed_moe_kernel(tc, xT, w_words, w_scales, gate, offs, out):
         def slot_offsets(first, count):
             return offsets[:, first // 16 : (first + count) // 16]
 
-        def gather_low(t, h):
-            nc.vector.tensor_copy(grouped[h][:, :, t], low[:, t, :].indirect(slot_offsets(h * HALF, HALF)))
+        def gather_low(t, first, count):
+            h, start = first // HALF, first % HALF
+            nc.vector.tensor_copy(
+                grouped[h][:, start : start + count, t], low[:, t, :].indirect(slot_offsets(first, count))
+            )
 
         def chunk_of_grouped(c):
             first = (c % 2) * CHUNK
@@ -78,9 +82,10 @@ def tile_routed_moe_kernel(tc, xT, w_words, w_scales, gate, offs, out):
                 chunk_of_grouped(c)[:, :, t], high[:, t - 2, :].indirect(slot_offsets(c * CHUNK, CHUNK)), COPY
             )
 
-        def quantize_and_multiply(c, codes):
+        def quantize_and_multiply(c, codes_of_half):
+            codes = codes_of_half[:, (c % 2) * CHUNK : (c % 2 + 1) * CHUNK]
             nc.vector.quantize_mx(
-                out=codes[:].bitcast(FP8X4),
+                out=codes.bitcast(FP8X4),
                 scales=scales[c][:],
                 in_=chunk_of_grouped(c).rearrange("p n t -> p (n t)"),
             )
@@ -105,41 +110,38 @@ def tile_routed_moe_kernel(tc, xT, w_words, w_scales, gate, offs, out):
                 MULT,
             )
 
+        sums = [held.tile([P, CHUNK], F32, name="sums%d" % c) for c in range(CHUNKS)]
+
         for h in range(2):
             nc.scalar.copy(high[:, 0, h * HALF : (h + 1) * HALF], staged[2, h][:])
-        gather_low(0, 0)
-        gather_low(0, 1)
-        nc.vector.tensor_copy(high[:, 1, 0:HALF], staged[3, 0][:])
+        gather_low(0, 0, HALF)
+        gather_low(0, HALF, HALF)
+        for h in range(2):
+            nc.vector.tensor_copy(high[:, 1, h * HALF : (h + 1) * HALF], staged[3, h][:])
         gather_high(2, 0)
-        nc.scalar.copy(high[:, 1, HALF:T], staged[3, 1][:])
-        gather_high(3, 0)
         gather_high(2, 1)
+        gather_high(3, 0)
         gather_high(3, 1)
-        gather_low(1, 0)
-        gather_low(1, 1)
+        gather_low(1, 0, CHUNK)
+        gather_low(1, CHUNK, CHUNK)
+        gather_low(1, 2 * CHUNK, CHUNK)
+        codes_a = held.tile([P, HALF], U32, name="codes_a", tag="codes", align_bytes=64)
+        quantize_and_multiply(0, codes_a)
+        gather_low(1, 3 * CHUNK, CHUNK)
+        nc.vector.tensor_copy(sums[0][:], banks[0][:])
         for c in (2, 3):
             gather_high(2, c)
             gather_high(3, c)
-
-        codes0 = held.tile([P, CHUNK], U32, name="codes0", align_bytes=64)
-        quantize_and_multiply(0, codes0)
-        codes1 = held.tile([P, CHUNK], U32, name="codes1", align_bytes=64)
-        quantize_and_multiply(1, codes1)
-        sums0 = held.tile([P, CHUNK], F32, name="sums0", tag="swap0", align_bytes=64)
-        nc.vector.tensor_copy(sums0[:], banks[0][:])
-        sums1 = held.tile([P, CHUNK], F32, name="sums1", tag="swap1", align_bytes=64)
-        nc.vector.tensor_copy(sums1[:], banks[1][:])
-        scatter(0, sums0)
-        codes2 = held.tile([P, CHUNK], U32, name="codes2", tag="swap0", align_bytes=64)
-        quantize_and_multiply(2, codes2)
-        scatter(1, sums1)
-        codes3 = held.tile([P, CHUNK], U32, name="codes3", tag="swap1", align_bytes=64)
-        quantize_and_multiply(3, codes3)
-        sums2 = held.tile([P, CHUNK], F32, name="sums2")
-        nc.scalar.copy(sums2[:], banks[2][:])
-        scatter(2, sums2)
-        sums3 = held.tile([P, CHUNK], F32, name="sums3")
-        nc.scalar.copy(sums3[:], banks[3][:])
-        scatter(3, sums3)
+        quantize_and_multiply(1, codes_a)
+        scatter(0, sums[0])
+        nc.vector.tensor_copy(sums[1][:], banks[1][:])
+        codes_b = held.tile([P, HALF], U32, name="codes_b", tag="codes", align_bytes=64)
+        quantize_and_multiply(2, codes_b)
+        scatter(1, sums[1])
+        quantize_and_multiply(3, codes_b)
+        nc.scalar.copy(sums[2][:], banks[2][:])
+        scatter(2, sums[2])
+        nc.scalar.copy(sums[3][:], banks[3][:])
+        scatter(3, sums[3])
 
         nc.sync.dma_start(out, window[:])

@@ -60,6 +60,7 @@ def tile_routed_moe_kernel(tc, xT, w_words, w_scales, gate, offs, out):
         window = held.tile([P, T], F32, name="window")
         high = held.tile([P, 2, T], BF16, name="high")
 
+        pairs = [held.tile([P, 2, HALF, 2], BF16, name="pairs%d" % h, align_bytes=64) for h in range(2)]
         grouped = [held.tile([P, HALF, PACK], BF16, name="grouped%d" % h, align_bytes=64) for h in range(2)]
         scales = [held.tile([P, CHUNK], U8, name="scales%d" % c, align_bytes=64) for c in range(CHUNKS)]
         banks = [psum.tile([P, CHUNK], F32, name="bank%d" % c) for c in range(CHUNKS)]
@@ -70,7 +71,7 @@ def tile_routed_moe_kernel(tc, xT, w_words, w_scales, gate, offs, out):
         def gather_low(t, first, count):
             h, start = first // HALF, first % HALF
             nc.vector.tensor_copy(
-                grouped[h][:, start : start + count, t], low[:, t, :].indirect(slot_offsets(first, count))
+                pairs[h][:, 0, start : start + count, t], low[:, t, :].indirect(slot_offsets(first, count))
             )
 
         def chunk_of_grouped(c):
@@ -78,9 +79,18 @@ def tile_routed_moe_kernel(tc, xT, w_words, w_scales, gate, offs, out):
             return grouped[c // 2][:, first : first + CHUNK, :]
 
         def gather_high(t, c):
+            first = (c % 2) * CHUNK
             nc.scalar.activation(
-                chunk_of_grouped(c)[:, :, t], high[:, t - 2, :].indirect(slot_offsets(c * CHUNK, CHUNK)), COPY
+                pairs[c // 2][:, 1, first : first + CHUNK, t - 2],
+                high[:, t - 2, :].indirect(slot_offsets(c * CHUNK, CHUNK)),
+                COPY,
             )
+
+        def merge(engine_copy, c):
+            first = (c % 2) * CHUNK
+            words_in = pairs[c // 2][:].rearrange("p u n e -> p (u n e)").bitcast(F32).rearrange("p (u n) -> p u n", u=2)
+            words_out = chunk_of_grouped(c).rearrange("p n t -> p (n t)").bitcast(F32).rearrange("p (n u) -> p n u", u=2)
+            engine_copy(words_out, words_in[:, :, first : first + CHUNK].rearrange("p u n -> p n u"))
 
         def quantize_and_multiply(c, codes_of_half):
             codes = codes_of_half[:, (c % 2) * CHUNK : (c % 2 + 1) * CHUNK]
@@ -124,6 +134,8 @@ def tile_routed_moe_kernel(tc, xT, w_words, w_scales, gate, offs, out):
         gather_high(3, 1)
         gather_low(1, 0, CHUNK)
         gather_low(1, CHUNK, CHUNK)
+        merge(nc.vector.tensor_copy, 0)
+        merge(nc.scalar.copy, 1)
         gather_low(1, 2 * CHUNK, CHUNK)
         codes_a = held.tile([P, HALF], U32, name="codes_a", tag="codes", align_bytes=64)
         quantize_and_multiply(0, codes_a)
@@ -132,6 +144,7 @@ def tile_routed_moe_kernel(tc, xT, w_words, w_scales, gate, offs, out):
         for c in (2, 3):
             gather_high(2, c)
             gather_high(3, c)
+            merge(nc.scalar.copy, c)
         quantize_and_multiply(1, codes_a)
         scatter(0, sums[0])
         nc.vector.tensor_copy(sums[1][:], banks[1][:])

@@ -29,73 +29,76 @@ def tile_routed_moe_kernel(tc, xT, w_words, w_scales, gate, offs, out):
         psum = ctx.enter_context(tc.psum_pool(name="psum", bufs=1))
 
         offsets = held.tile([P, E * C // 16], U16, name="offsets")
-        nc.sync.dma_start(offsets[:], offs)
-
         x_view = xT.rearrange("(p t) n -> p t n", t=PACK)
         low = held.tile([P, 2, T], F32, name="low")
         staged = {}
-        nc.sync.dma_start(low[:, 0, :], x_view[:, 0, :])
         for t in (2, 3):
             for h in range(2):
-                staged[t, h] = held.tile([P, HALF], F32, name="staged%d_%d" % (t, h))
-                nc.sync.dma_start(staged[t, h][:], x_view[:, t, h * HALF : (h + 1) * HALF])
-        nc.sync.dma_start(low[:, 1, :], x_view[:, 1, :])
-
+                staged[t, h] = held.tile([P, HALF], F32, name="staged%d_%d" % (t, h), tag="staged%d_%d" % (t, h), align_bytes=64)
         w_planes = held.tile([P, E, N], U8, name="w_planes", align_bytes=64)
+        w_codes = held.tile([P, E, N], U32, name="w_codes", align_bytes=64)
+        gate_sb = held.tile([P, E * C], F32, name="gate_sb")
+
+        nc.sync.dma_start(low[:, 0, :], x_view[:, 0, :])
+        nc.sync.dma_start(offsets[:], offs)
+        nc.sync.dma_start(staged[2, 0][:], x_view[:, 2, 0 * HALF : 1 * HALF])
+        nc.sync.dma_start(staged[2, 1][:], x_view[:, 2, 1 * HALF : 2 * HALF])
+        nc.sync.dma_start(staged[3, 0][:], x_view[:, 3, 0 * HALF : 1 * HALF])
+        nc.sync.dma_start(staged[3, 1][:], x_view[:, 3, 1 * HALF : 2 * HALF])
+        nc.sync.dma_start(low[:, 1, :], x_view[:, 1, :])
         nc.vector.memset(w_planes[:].rearrange("p e n -> p (e n)").bitcast(I32), 0)
         for q in range(4):
             nc.sync.dma_start(
                 w_planes[32 * q : 32 * q + 4, :, :].bitcast(I32),
                 w_scales[:, 0, 4 * q : 4 * q + 4, :].rearrange("e r n -> r e n").bitcast(I32),
             )
-        gate_sb = held.tile([P, E * C], F32, name="gate_sb")
-        nc.sync.dma_start(gate_sb[:, 0:CHUNK], gate[:, 0:CHUNK])
-        w_codes = held.tile([P, E, N], U32, name="w_codes", align_bytes=64)
         nc.sync.dma_start(
             w_codes[:].bitcast(I32),
             w_words.rearrange("e a p n r -> p (e a) (n r)").bitcast(I32),
         )
+        nc.sync.dma_start(gate_sb[:, 0:CHUNK], gate[:, 0:CHUNK])
         nc.sync.dma_start(gate_sb[:, CHUNK : E * C], gate[:, CHUNK : E * C])
 
         window = held.tile([P, T], F32, name="window")
         high = held.tile([P, 2, T], BF16, name="high")
 
-        pairs = [held.tile([P, 2, HALF, 2], BF16, name="pairs%d" % h, align_bytes=64) for h in range(2)]
+        lanes = [held.tile([P, 3 * CHUNK, 2], BF16, name="lane%d" % i, tag="lane%d" % i, align_bytes=64) for i in range(2)]
         grouped = [held.tile([P, HALF, PACK], BF16, name="grouped%d" % h, align_bytes=64) for h in range(2)]
         scales = [held.tile([P, CHUNK], U8, name="scales%d" % c, align_bytes=64) for c in range(CHUNKS)]
         banks = [psum.tile([P, CHUNK], F32, name="bank%d" % c) for c in range(CHUNKS)]
+        sums = {}
+        codes = {}
 
-        def slot_offsets(first, count):
-            return offsets[:, first // 16 : (first + count) // 16]
+        def slot_offsets(c):
+            return offsets[:, c * CHUNK // 16 : (c + 1) * CHUNK // 16]
 
-        def gather_low(t, first, count):
-            h, start = first // HALF, first % HALF
-            nc.vector.tensor_copy(
-                pairs[h][:, 0, start : start + count, t], low[:, t, :].indirect(slot_offsets(first, count))
+        def gather_low(t, c):
+            first = (1 - c // 2) * CHUNK
+            nc.vector.tensor_copy(lanes[c % 2][:, first : first + CHUNK, t], low[:, t, :].indirect(slot_offsets(c)))
+
+        def gather_high(t, c, first=0, count=CHUNK):
+            nc.scalar.activation(
+                lanes[c % 2][:, 2 * CHUNK + first : 2 * CHUNK + first + count, t - 2],
+                high[:, t - 2, :].indirect(offsets[:, (c * CHUNK + first) // 16 : (c * CHUNK + first + count) // 16]),
+                COPY,
             )
 
         def chunk_of_grouped(c):
             first = (c % 2) * CHUNK
             return grouped[c // 2][:, first : first + CHUNK, :]
 
-        def gather_high(t, c):
-            first = (c % 2) * CHUNK
-            nc.scalar.activation(
-                pairs[c // 2][:, 1, first : first + CHUNK, t - 2],
-                high[:, t - 2, :].indirect(slot_offsets(c * CHUNK, CHUNK)),
-                COPY,
-            )
-
         def merge(engine_copy, c):
-            first = (c % 2) * CHUNK
-            words_in = pairs[c // 2][:].rearrange("p u n e -> p (u n e)").bitcast(F32).rearrange("p (u n) -> p u n", u=2)
+            blocks = lanes[c % 2][:].rearrange("p n e -> p (n e)").bitcast(F32).rearrange("p (b n) -> p b n", n=CHUNK)
+            words_in = blocks[:, 1 - c // 2 : 3 : 1 + c // 2, :]
             words_out = chunk_of_grouped(c).rearrange("p n t -> p (n t)").bitcast(F32).rearrange("p (n u) -> p n u", u=2)
-            engine_copy(words_out, words_in[:, :, first : first + CHUNK].rearrange("p u n -> p n u"))
+            engine_copy(words_out, words_in.rearrange("p u n -> p n u"))
 
-        def quantize_and_multiply(c, codes_of_half):
-            codes = codes_of_half[:, (c % 2) * CHUNK : (c % 2 + 1) * CHUNK]
+        def quantize_and_multiply(c):
+            if c % 2 == 0:
+                codes[c // 2] = held.tile([P, HALF], U32, name="codes%d" % (c // 2), tag="codes", align_bytes=64)
+            words = codes[c // 2][:, (c % 2) * CHUNK : (c % 2 + 1) * CHUNK]
             nc.vector.quantize_mx(
-                out=codes.bitcast(FP8X4),
+                out=words.bitcast(FP8X4),
                 scales=scales[c][:],
                 in_=chunk_of_grouped(c).rearrange("p n t -> p (n t)"),
             )
@@ -106,55 +109,54 @@ def tile_routed_moe_kernel(tc, xT, w_words, w_scales, gate, offs, out):
                     out=banks[c][:, cols],
                     lhsT=w_codes[:, e, :].bitcast(FP8X4),
                     lhsT_scale=w_planes[:, e, :],
-                    rhs=codes[:, cols].bitcast(FP8X4),
+                    rhs=words[:, cols].bitcast(FP8X4),
                     rhs_scale=scales[c][:, cols],
                     start=True,
                     stop=True,
                 )
 
-        def scatter(c, sums):
-            nc.vector.tensor_tensor(
-                window[:].indirect(slot_offsets(c * CHUNK, CHUNK)),
-                sums[:],
-                gate_sb[:, c * CHUNK : (c + 1) * CHUNK],
-                MULT,
-            )
+        def empty_bank(engine_copy, c, tag):
+            sums[c] = held.tile([P, CHUNK], F32, name="sums%d" % c, tag=tag, align_bytes=64)
+            engine_copy(sums[c][:], banks[c][:])
 
-        sums = [held.tile([P, CHUNK], F32, name="sums%d" % c) for c in range(CHUNKS)]
+        def scatter(c):
+            nc.vector.tensor_tensor(window[:].indirect(slot_offsets(c)), sums[c][:], gate_sb[:, c * CHUNK : (c + 1) * CHUNK], MULT)
 
-        for h in range(2):
-            nc.scalar.copy(high[:, 0, h * HALF : (h + 1) * HALF], staged[2, h][:])
-        gather_low(0, 0, HALF)
-        gather_low(0, HALF, HALF)
-        for h in range(2):
-            nc.vector.tensor_copy(high[:, 1, h * HALF : (h + 1) * HALF], staged[3, h][:])
+        nc.scalar.copy(high[:, 0, 0 * HALF : 1 * HALF], staged[2, 0][:])
+        nc.scalar.copy(high[:, 0, 1 * HALF : 2 * HALF], staged[2, 1][:])
+        gather_low(0, 0)
+        gather_low(0, 1)
+        gather_low(0, 2)
+        gather_low(0, 3)
+        nc.vector.tensor_copy(high[:, 1, 0 * HALF : 1 * HALF], staged[3, 0][:])
+        nc.vector.tensor_copy(high[:, 1, 1 * HALF : 2 * HALF], staged[3, 1][:])
         gather_high(2, 0)
         gather_high(2, 1)
         gather_high(3, 0)
         gather_high(3, 1)
-        gather_low(1, 0, CHUNK)
-        gather_low(1, CHUNK, CHUNK)
-        merge(nc.vector.tensor_copy, 0)
+        gather_low(1, 0)
+        merge(nc.scalar.copy, 0)
+        gather_low(1, 1)
         merge(nc.scalar.copy, 1)
-        gather_low(1, 2 * CHUNK, CHUNK)
-        codes_a = held.tile([P, HALF], U32, name="codes_a", tag="codes", align_bytes=64)
-        quantize_and_multiply(0, codes_a)
-        gather_low(1, 3 * CHUNK, CHUNK)
-        nc.vector.tensor_copy(sums[0][:], banks[0][:])
-        for c in (2, 3):
-            gather_high(2, c)
-            gather_high(3, c)
-            merge(nc.scalar.copy, c)
-        quantize_and_multiply(1, codes_a)
-        scatter(0, sums[0])
-        nc.vector.tensor_copy(sums[1][:], banks[1][:])
-        codes_b = held.tile([P, HALF], U32, name="codes_b", tag="codes", align_bytes=64)
-        quantize_and_multiply(2, codes_b)
-        scatter(1, sums[1])
-        quantize_and_multiply(3, codes_b)
-        nc.scalar.copy(sums[2][:], banks[2][:])
-        scatter(2, sums[2])
-        nc.scalar.copy(sums[3][:], banks[3][:])
-        scatter(3, sums[3])
+        gather_low(1, 2)
+        quantize_and_multiply(0)
+        gather_low(1, 3)
+        quantize_and_multiply(1)
+        empty_bank(nc.vector.tensor_copy, 0, "sums0")
+        gather_high(2, 2)
+        gather_high(3, 2)
+        gather_high(2, 3)
+        merge(nc.scalar.copy, 2)
+        scatter(0)
+        empty_bank(nc.scalar.copy, 1, "sums1")
+        quantize_and_multiply(2)
+        gather_high(3, 3)
+        merge(nc.scalar.copy, 3)
+        scatter(1)
+        quantize_and_multiply(3)
+        empty_bank(nc.scalar.copy, 2, "lane1")
+        scatter(2)
+        empty_bank(nc.scalar.copy, 3, "sums3")
+        scatter(3)
 
         nc.sync.dma_start(out, window[:])

@@ -19,6 +19,7 @@ P = 128
 PACK = 4
 CHUNK = 512
 CHUNKS = E * C // CHUNK
+ORDER = (0, 2, 1, 3)
 HALF = T // 2
 
 
@@ -69,17 +70,18 @@ def tile_routed_moe_kernel(tc, xT, w_words, w_scales, gate, offs, out):
         sums = {}
         codes = {}
 
-        def slot_offsets(c):
-            return offsets[:, c * CHUNK // 16 : (c + 1) * CHUNK // 16]
+        def slot_offsets(s, count=CHUNK):
+            first = ORDER[s] * CHUNK
+            return offsets[:, first // 16 : (first + count) // 16]
 
-        def gather_low(t, c):
-            first = (1 - c // 2) * CHUNK
-            nc.vector.tensor_copy(lanes[c % 2][:, first : first + CHUNK, t], low[:, t, :].indirect(slot_offsets(c)))
+        def gather_low(t, s, count=CHUNK):
+            first = (s // 2) * CHUNK
+            nc.vector.tensor_copy(lanes[s % 2][:, first : first + count, t], low[:, t, :].indirect(slot_offsets(s, count)))
 
         def gather_high(t, c, first=0, count=CHUNK):
             nc.scalar.activation(
                 lanes[c % 2][:, 2 * CHUNK + first : 2 * CHUNK + first + count, t - 2],
-                high[:, t - 2, :].indirect(offsets[:, (c * CHUNK + first) // 16 : (c * CHUNK + first + count) // 16]),
+                high[:, t - 2, :].indirect(offsets[:, (ORDER[c] * CHUNK + first) // 16 : (ORDER[c] * CHUNK + first + count) // 16]),
                 COPY,
             )
 
@@ -89,7 +91,7 @@ def tile_routed_moe_kernel(tc, xT, w_words, w_scales, gate, offs, out):
 
         def merge(engine_copy, c):
             blocks = lanes[c % 2][:].rearrange("p n e -> p (n e)").bitcast(F32).rearrange("p (b n) -> p b n", n=CHUNK)
-            words_in = blocks[:, 1 - c // 2 : 3 : 1 + c // 2, :]
+            words_in = blocks[:, c // 2 : 3 : 2 - c // 2, :]
             words_out = chunk_of_grouped(c).rearrange("p n t -> p (n t)").bitcast(F32).rearrange("p (n u) -> p n u", u=2)
             engine_copy(words_out, words_in.rearrange("p u n -> p n u"))
 
@@ -103,7 +105,7 @@ def tile_routed_moe_kernel(tc, xT, w_words, w_scales, gate, offs, out):
                 in_=chunk_of_grouped(c).rearrange("p n t -> p (n t)"),
             )
             for h in range(CHUNK // C):
-                e = c * (CHUNK // C) + h
+                e = ORDER[c] * (CHUNK // C) + h
                 cols = slice(h * C, (h + 1) * C)
                 nc.tensor.matmul_mx(
                     out=banks[c][:, cols],
@@ -120,14 +122,12 @@ def tile_routed_moe_kernel(tc, xT, w_words, w_scales, gate, offs, out):
             engine_copy(sums[c][:], banks[c][:])
 
         def scatter(c):
-            nc.vector.tensor_tensor(window[:].indirect(slot_offsets(c)), sums[c][:], gate_sb[:, c * CHUNK : (c + 1) * CHUNK], MULT)
+            nc.vector.tensor_tensor(window[:].indirect(slot_offsets(c)), sums[c][:], gate_sb[:, ORDER[c] * CHUNK : (ORDER[c] + 1) * CHUNK], MULT)
 
         nc.scalar.copy(high[:, 0, 0 * HALF : 1 * HALF], staged[2, 0][:])
         nc.scalar.copy(high[:, 0, 1 * HALF : 2 * HALF], staged[2, 1][:])
-        gather_low(0, 0)
-        gather_low(0, 1)
-        gather_low(0, 2)
-        gather_low(0, 3)
+        gather_low(0, 0, 2 * CHUNK)
+        gather_low(0, 1, 2 * CHUNK)
         nc.vector.tensor_copy(high[:, 1, 0 * HALF : 1 * HALF], staged[3, 0][:])
         nc.vector.tensor_copy(high[:, 1, 1 * HALF : 2 * HALF], staged[3, 1][:])
         gather_high(2, 0)

@@ -32,20 +32,17 @@ def tile_routed_moe_kernel(tc, xT, w_words, w_scales, gate, offs, out):
         offsets = held.tile([P, E * C // 16], U16, name="offsets")
         x_view = xT.rearrange("(p t) n -> p t n", t=PACK)
         low = held.tile([P, 2, T], F32, name="low")
-        staged = {}
-        for t in (2, 3):
-            for h in range(2):
-                staged[t, h] = held.tile([P, HALF], F32, name="staged%d_%d" % (t, h), tag="staged%d_%d" % (t, h), align_bytes=64)
+        staged2 = [held.tile([P, HALF], F32, name="staged2_%d" % h) for h in range(2)]
+        staged3 = held.tile([P, T], F32, name="staged3")
         w_planes = held.tile([P, E, N], U8, name="w_planes", align_bytes=64)
         w_codes = held.tile([P, E, N], U32, name="w_codes", align_bytes=64)
         gate_sb = held.tile([P, E * C], F32, name="gate_sb")
 
         nc.sync.dma_start(low[:, 0, :], x_view[:, 0, :])
         nc.sync.dma_start(offsets[:], offs)
-        nc.sync.dma_start(staged[2, 0][:], x_view[:, 2, 0 * HALF : 1 * HALF])
-        nc.sync.dma_start(staged[2, 1][:], x_view[:, 2, 1 * HALF : 2 * HALF])
-        nc.sync.dma_start(staged[3, 0][:], x_view[:, 3, 0 * HALF : 1 * HALF])
-        nc.sync.dma_start(staged[3, 1][:], x_view[:, 3, 1 * HALF : 2 * HALF])
+        for h in range(2):
+            nc.sync.dma_start(staged2[h][:], x_view[:, 2, h * HALF : (h + 1) * HALF])
+        nc.sync.dma_start(staged3[:], x_view[:, 3, :])
         nc.sync.dma_start(low[:, 1, :], x_view[:, 1, :])
         nc.vector.memset(w_planes[:].rearrange("p e n -> p (e n)").bitcast(I32), 0)
         for q in range(4):
@@ -97,7 +94,7 @@ def tile_routed_moe_kernel(tc, xT, w_words, w_scales, gate, offs, out):
 
         def quantize_and_multiply(c):
             if c % 2 == 0:
-                codes[c // 2] = held.tile([P, HALF], U32, name="codes%d" % (c // 2), tag="codes", align_bytes=64)
+                codes[c // 2] = held.tile([P, HALF], U32, name="codes%d" % (c // 2), tag="codes%d" % (c // 2), align_bytes=64)
             words = codes[c // 2][:, (c % 2) * CHUNK : (c % 2 + 1) * CHUNK]
             nc.vector.quantize_mx(
                 out=words.bitcast(FP8X4),
@@ -124,12 +121,11 @@ def tile_routed_moe_kernel(tc, xT, w_words, w_scales, gate, offs, out):
         def scatter(c):
             nc.vector.tensor_tensor(window[:].indirect(slot_offsets(c)), sums[c][:], gate_sb[:, ORDER[c] * CHUNK : (ORDER[c] + 1) * CHUNK], MULT)
 
-        nc.scalar.copy(high[:, 0, 0 * HALF : 1 * HALF], staged[2, 0][:])
-        nc.scalar.copy(high[:, 0, 1 * HALF : 2 * HALF], staged[2, 1][:])
+        for h in range(2):
+            nc.scalar.copy(high[:, 0, h * HALF : (h + 1) * HALF], staged2[h][:])
         gather_low(0, 0, 2 * CHUNK)
         gather_low(0, 1, 2 * CHUNK)
-        nc.vector.tensor_copy(high[:, 1, 0 * HALF : 1 * HALF], staged[3, 0][:])
-        nc.vector.tensor_copy(high[:, 1, 1 * HALF : 2 * HALF], staged[3, 1][:])
+        nc.vector.tensor_copy(high[:, 1, :], staged3[:])
         gather_high(2, 0)
         gather_high(2, 1)
         gather_high(3, 0)
@@ -154,7 +150,7 @@ def tile_routed_moe_kernel(tc, xT, w_words, w_scales, gate, offs, out):
         merge(nc.scalar.copy, 3)
         scatter(1)
         quantize_and_multiply(3)
-        empty_bank(nc.scalar.copy, 2, "lane1")
+        empty_bank(nc.scalar.copy, 2, "sums2")
         scatter(2)
         empty_bank(nc.scalar.copy, 3, "sums3")
         scatter(3)

@@ -19,7 +19,6 @@ P = 128
 PACK = 4
 CHUNK = 512
 CHUNKS = E * C // CHUNK
-ORDER = (0, 2, 1, 3)
 HALF = T // 2
 
 
@@ -60,49 +59,47 @@ def tile_routed_moe_kernel(tc, xT, w_words, w_scales, gate, offs, out):
         window = held.tile([P, T], F32, name="window")
         high = held.tile([P, 2, T], BF16, name="high")
 
-        lanes = [held.tile([P, 3 * CHUNK, 2], BF16, name="lane%d" % i, tag="lane%d" % i, align_bytes=64) for i in range(2)]
+        pairs = held.tile([P, 6 * CHUNK, 2], BF16, name="pairs", align_bytes=64)
         grouped = [held.tile([P, HALF, PACK], BF16, name="grouped%d" % h, align_bytes=64) for h in range(2)]
         scales = [held.tile([P, CHUNK], U8, name="scales%d" % c, align_bytes=64) for c in range(CHUNKS)]
         banks = [psum.tile([P, CHUNK], F32, name="bank%d" % c) for c in range(CHUNKS)]
         sums = {}
         codes = {}
 
-        def slot_offsets(s, count=CHUNK):
-            first = ORDER[s] * CHUNK
-            return offsets[:, first // 16 : (first + count) // 16]
+        def slot_offsets(c, chunks=1):
+            return offsets[:, c * CHUNK // 16 : (c + chunks) * CHUNK // 16]
 
-        def gather_low(t, s, count=CHUNK):
-            first = (s // 2) * CHUNK
-            nc.vector.tensor_copy(lanes[s % 2][:, first : first + count, t], low[:, t, :].indirect(slot_offsets(s, count)))
+        def gather_low(t, c, chunks=1):
+            nc.vector.tensor_copy(pairs[:, c * CHUNK : (c + chunks) * CHUNK, t], low[:, t, :].indirect(slot_offsets(c, chunks)))
 
-        def gather_high(t, c, first=0, count=CHUNK):
-            nc.scalar.activation(
-                lanes[c % 2][:, 2 * CHUNK + first : 2 * CHUNK + first + count, t - 2],
-                high[:, t - 2, :].indirect(offsets[:, (ORDER[c] * CHUNK + first) // 16 : (ORDER[c] * CHUNK + first + count) // 16]),
-                COPY,
-            )
+        def gather_high(t, c, chunks=1):
+            first = (4 + c % 2) * CHUNK
+            nc.scalar.activation(pairs[:, first : first + chunks * CHUNK, t - 2], high[:, t - 2, :].indirect(slot_offsets(c, chunks)), COPY)
 
         def chunk_of_grouped(c):
             first = (c % 2) * CHUNK
             return grouped[c // 2][:, first : first + CHUNK, :]
 
         def merge(engine_copy, c):
-            blocks = lanes[c % 2][:].rearrange("p n e -> p (n e)").bitcast(F32).rearrange("p (b n) -> p b n", n=CHUNK)
-            words_in = blocks[:, c // 2 : 3 : 2 - c // 2, :]
+            blocks = pairs[:].rearrange("p n e -> p (n e)").bitcast(F32).rearrange("p (b n) -> p b n", n=CHUNK)
+            words_in = blocks[:, c : 5 + c % 2 : 4 + c % 2 - c, :]
             words_out = chunk_of_grouped(c).rearrange("p n t -> p (n t)").bitcast(F32).rearrange("p (n u) -> p n u", u=2)
             engine_copy(words_out, words_in.rearrange("p u n -> p n u"))
 
-        def quantize_and_multiply(c):
+        def quantize_and_multiply(c, pieces=1):
             if c % 2 == 0:
                 codes[c // 2] = held.tile([P, HALF], U32, name="codes%d" % (c // 2), tag="codes%d" % (c // 2), align_bytes=64)
             words = codes[c // 2][:, (c % 2) * CHUNK : (c % 2 + 1) * CHUNK]
-            nc.vector.quantize_mx(
-                out=words.bitcast(FP8X4),
-                scales=scales[c][:],
-                in_=chunk_of_grouped(c).rearrange("p n t -> p (n t)"),
-            )
+            values = chunk_of_grouped(c).rearrange("p n t -> p (n t)")
+            width = CHUNK // pieces
+            for i in range(pieces):
+                nc.vector.quantize_mx(
+                    out=words[:, i * width : (i + 1) * width].bitcast(FP8X4),
+                    scales=scales[c][:, i * width : (i + 1) * width],
+                    in_=values[:, i * width * PACK : (i + 1) * width * PACK],
+                )
             for h in range(CHUNK // C):
-                e = ORDER[c] * (CHUNK // C) + h
+                e = c * (CHUNK // C) + h
                 cols = slice(h * C, (h + 1) * C)
                 nc.tensor.matmul_mx(
                     out=banks[c][:, cols],
@@ -119,24 +116,20 @@ def tile_routed_moe_kernel(tc, xT, w_words, w_scales, gate, offs, out):
             engine_copy(sums[c][:], banks[c][:])
 
         def scatter(c):
-            nc.vector.tensor_tensor(window[:].indirect(slot_offsets(c)), sums[c][:], gate_sb[:, ORDER[c] * CHUNK : (ORDER[c] + 1) * CHUNK], MULT)
+            nc.vector.tensor_tensor(window[:].indirect(slot_offsets(c)), sums[c][:], gate_sb[:, c * CHUNK : (c + 1) * CHUNK], MULT)
 
         for h in range(2):
             nc.scalar.copy(high[:, 0, h * HALF : (h + 1) * HALF], staged2[h][:])
-        gather_low(0, 0, 2 * CHUNK)
-        gather_low(0, 1, 2 * CHUNK)
+        gather_low(0, 0, 2)
+        gather_low(0, 2, 2)
         nc.vector.tensor_copy(high[:, 1, :], staged3[:])
-        gather_high(2, 0)
-        gather_high(2, 1)
-        gather_high(3, 0)
-        gather_high(3, 1)
-        gather_low(1, 0)
+        gather_high(2, 0, 2)
+        gather_high(3, 0, 2)
+        gather_low(1, 0, 2)
         merge(nc.scalar.copy, 0)
-        gather_low(1, 1)
         merge(nc.scalar.copy, 1)
-        gather_low(1, 2)
-        quantize_and_multiply(0)
-        gather_low(1, 3)
+        gather_low(1, 2, 2)
+        quantize_and_multiply(0, 2)
         quantize_and_multiply(1)
         empty_bank(nc.vector.tensor_copy, 0, "sums0")
         gather_high(2, 2)

from contextlib import ExitStack

import concourse.mybir as mybir

K, T, E, C, N = 512, 2048, 8, 256, 128
FLOPS = 2 * K * N * E * C

F32 = mybir.dt.float32
BF16 = mybir.dt.bfloat16
U32 = mybir.dt.uint32
I32 = mybir.dt.int32
U16 = mybir.dt.uint16
U8 = mybir.dt.uint8
FP8X4 = mybir.dt.float8_e4m3fn_x4
MULT = mybir.AluOpType.mult
COPY = mybir.ActivationFunctionType.Copy

P = 128
PACK = 4
CHUNK = 512
CHUNKS = E * C // CHUNK
HALF = T // 2


def tile_routed_moe_kernel(tc, xT, w_words, w_scales, gate, offs, out):
    nc = tc.nc
    with ExitStack() as ctx:
        held = ctx.enter_context(tc.tile_pool(name="held", bufs=1))
        psum = ctx.enter_context(tc.psum_pool(name="psum", bufs=1))

        offsets = held.tile([P, E * C // 16], U16, name="offsets")
        x_view = xT.rearrange("(p t) n -> p t n", t=PACK)
        low = held.tile([P, 2, T], F32, name="low")
        staged2 = [held.tile([P, HALF], F32, name="staged2_%d" % h) for h in range(2)]
        staged3 = held.tile([P, T], F32, name="staged3")
        w_planes = held.tile([P, E, N], U8, name="w_planes", align_bytes=64)
        w_codes = held.tile([P, E, N], U32, name="w_codes", align_bytes=64)
        gate_sb = held.tile([P, E * C], F32, name="gate_sb")

        nc.sync.dma_start(low[:, 0, :], x_view[:, 0, :])
        nc.sync.dma_start(offsets[:], offs)
        for h in range(2):
            nc.sync.dma_start(staged2[h][:], x_view[:, 2, h * HALF : (h + 1) * HALF])
        nc.sync.dma_start(staged3[:], x_view[:, 3, :])
        nc.sync.dma_start(low[:, 1, :], x_view[:, 1, :])
        nc.vector.memset(w_planes[:].rearrange("p e n -> p (e n)").bitcast(I32), 0)
        for q in range(4):
            nc.sync.dma_start(
                w_planes[32 * q : 32 * q + 4, :, :].bitcast(I32),
                w_scales[:, 0, 4 * q : 4 * q + 4, :].rearrange("e r n -> r e n").bitcast(I32),
            )
        nc.sync.dma_start(
            w_codes[:].bitcast(I32),
            w_words.rearrange("e a p n r -> p (e a) (n r)").bitcast(I32),
        )
        nc.sync.dma_start(gate_sb[:, 0:CHUNK], gate[:, 0:CHUNK])
        nc.sync.dma_start(gate_sb[:, CHUNK : E * C], gate[:, CHUNK : E * C])

        window = held.tile([P, T], F32, name="window")
        high = held.tile([P, 2, T], BF16, name="high")

        pairs = held.tile([P, 6 * CHUNK, 2], BF16, name="pairs", align_bytes=64)
        grouped = [held.tile([P, HALF, PACK], BF16, name="grouped%d" % h, align_bytes=64) for h in range(2)]
        scales = [held.tile([P, CHUNK], U8, name="scales%d" % c, align_bytes=64) for c in range(CHUNKS)]
        banks = [psum.tile([P, CHUNK], F32, name="bank%d" % c) for c in range(CHUNKS)]
        sums = {}
        codes = {}

        def slot_offsets(c, chunks=1):
            return offsets[:, c * CHUNK // 16 : (c + chunks) * CHUNK // 16]

        def gather_low(t, c, chunks=1):
            nc.vector.tensor_copy(pairs[:, c * CHUNK : (c + chunks) * CHUNK, t], low[:, t, :].indirect(slot_offsets(c, chunks)))

        def gather_high(t, c, chunks=1):
            first = (4 + c % 2) * CHUNK
            nc.scalar.activation(pairs[:, first : first + chunks * CHUNK, t - 2], high[:, t - 2, :].indirect(slot_offsets(c, chunks)), COPY)

        def chunk_of_grouped(c):
            first = (c % 2) * CHUNK
            return grouped[c // 2][:, first : first + CHUNK, :]

        def merge(engine_copy, c):
            blocks = pairs[:].rearrange("p n e -> p (n e)").bitcast(F32).rearrange("p (b n) -> p b n", n=CHUNK)
            words_in = blocks[:, c : 5 + c % 2 : 4 + c % 2 - c, :]
            words_out = chunk_of_grouped(c).rearrange("p n t -> p (n t)").bitcast(F32).rearrange("p (n u) -> p n u", u=2)
            engine_copy(words_out, words_in.rearrange("p u n -> p n u"))

        def quantize_and_multiply(c, pieces=1):
            if c % 2 == 0:
                codes[c // 2] = held.tile([P, HALF], U32, name="codes%d" % (c // 2), tag="codes%d" % (c // 2), align_bytes=64)
            words = codes[c // 2][:, (c % 2) * CHUNK : (c % 2 + 1) * CHUNK]
            values = chunk_of_grouped(c).rearrange("p n t -> p (n t)")
            width = CHUNK // pieces
            for i in range(pieces):
                nc.vector.quantize_mx(
                    out=words[:, i * width : (i + 1) * width].bitcast(FP8X4),
                    scales=scales[c][:, i * width : (i + 1) * width],
                    in_=values[:, i * width * PACK : (i + 1) * width * PACK],
                )
            for h in range(CHUNK // C):
                e = c * (CHUNK // C) + h
                cols = slice(h * C, (h + 1) * C)
                nc.tensor.matmul_mx(
                    out=banks[c][:, cols],
                    lhsT=w_codes[:, e, :].bitcast(FP8X4),
                    lhsT_scale=w_planes[:, e, :],
                    rhs=words[:, cols].bitcast(FP8X4),
                    rhs_scale=scales[c][:, cols],
                    start=True,
                    stop=True,
                )

        def empty_bank(engine_copy, c, tag):
            sums[c] = held.tile([P, CHUNK], F32, name="sums%d" % c, tag=tag, align_bytes=64)
            engine_copy(sums[c][:], banks[c][:])

        def scatter(c):
            nc.vector.tensor_tensor(window[:].indirect(slot_offsets(c)), sums[c][:], gate_sb[:, c * CHUNK : (c + 1) * CHUNK], MULT)

        for h in range(2):
            nc.scalar.copy(high[:, 0, h * HALF : (h + 1) * HALF], staged2[h][:])
        gather_low(0, 0, 2)
        gather_low(0, 2, 2)
        nc.vector.tensor_copy(high[:, 1, :], staged3[:])
        gather_high(2, 0, 2)
        gather_high(3, 0, 2)
        gather_low(1, 0, 2)
        merge(nc.scalar.copy, 0)
        merge(nc.scalar.copy, 1)
        gather_low(1, 2, 2)
        quantize_and_multiply(0, 2)
        quantize_and_multiply(1)
        empty_bank(nc.vector.tensor_copy, 0, "sums0")
        gather_high(2, 2)
        gather_high(3, 2)
        gather_high(2, 3)
        merge(nc.scalar.copy, 2)
        scatter(0)
        empty_bank(nc.scalar.copy, 1, "sums1")
        quantize_and_multiply(2)
        gather_high(3, 3)
        merge(nc.scalar.copy, 3)
        scatter(1)
        quantize_and_multiply(3)
        empty_bank(nc.scalar.copy, 2, "sums2")
        scatter(2)
        empty_bank(nc.scalar.copy, 3, "sums3")
        scatter(3)

        nc.sync.dma_start(out, window[:])
